import numpy as np
import ml_dtypes


def mxq(x, axis, fmt="e4m3"):
    dtype, down = {"e4m3": (ml_dtypes.float8_e4m3fn, 7), "e5m2": (ml_dtypes.float8_e5m2, 14)}[fmt]
    v = np.moveaxis(np.asarray(x, np.float32).astype(ml_dtypes.bfloat16).astype(np.float64), axis, -1)
    blocks = v.reshape(v.shape[:-1] + (-1, 32))
    amax = np.abs(blocks).max(-1, keepdims=True)
    byte = np.maximum(np.where(amax > 0, np.frexp(amax)[1] - 1 + 127, 0) - down, 1)
    scale = np.exp2(byte - 127.0)
    codes = (blocks / scale).astype(np.float32).astype(dtype).astype(np.float64)
    return np.moveaxis((codes * scale).reshape(v.shape), -1, axis)


WIDE = False


def mx_kscale(k):
    if not WIDE:
        return np.ones(k)
    levels = np.array([10, -10, 5, -5, 0])
    if k % 512:
        return np.exp2(np.random.permutation(np.resize(levels, k // 32))).repeat(32)
    a = np.empty((k // 512, 16))
    for p in range(k // 512):
        a[p, :8] = np.random.permutation(np.resize(levels, 8))
        for g in range(8):
            far = levels[np.abs(levels - a[p, g]) >= 10]
            a[p, g + 8] = far[np.random.randint(len(far))]
    return np.exp2(a.ravel()).repeat(32)


def f64(x):
    return np.asarray(x).astype(np.float64)


def striped(idx):
    return np.tile(idx.reshape(-1, 16).T, (8, 1)).astype(np.uint16)


def unstriped(offs):
    return offs[:16].T.reshape(-1).astype(np.int64)

def planes(y):
    n, m = y.shape
    v = y.astype(np.float32).astype(ml_dtypes.bfloat16).astype(np.float64).reshape(n // 32, 32, m)
    top = np.abs(v).max(1)
    byte = np.clip(np.where(top > 0, np.frexp(top)[1] - 1 + 127 - 7, 1), 1, 254)
    codes = (v * np.exp2(127.0 - byte)[:, None, :]).reshape(n, m).astype(np.float32).astype(ml_dtypes.float8_e4m3fn).view(np.uint8)
    words = codes.reshape(n // 512, 128, 4, m).transpose(0, 1, 3, 2)
    return np.ascontiguousarray(words), np.ascontiguousarray(byte.astype(np.uint8).reshape(n // 512, 16, m))


K, T, S, V, N = 512, 1024, 512, 256, 512
P = 2 ** 7


def setup_inputs():
    n = np.random.standard_normal
    s = mx_kscale(K)[:, None]
    return {
        "xT": (n((K, T)) * s).astype(np.float32),
        "w1": (n((K, N)) / np.sqrt(K) / s).astype(np.float32),
        "bound": np.tile(np.random.uniform(0.3, 1.2, V), (P, 1)).astype(np.float32),
        "offs": striped(np.random.permutation(T)[:S]),
        "cen": striped(np.random.permutation(S)[:V]),
        "pos1": striped(np.random.permutation(S)[:V]),
        "pos2": striped(np.random.permutation(S)[:V]),
        "pos3": striped(np.random.permutation(S)[:V]),
        "pos4": striped(np.random.permutation(S)[:V]),
    }


def reference(xT, w1, bound, offs, cen, pos1, pos2, pos3, pos4):
    xq = mxq(f64(xT)[:, unstriped(offs)], 0, "e4m3")
    y = mxq(f64(w1), 0, "e4m3").T @ xq
    yc = y[:, unstriped(cen)]
    low = -1.0 * f64(bound)[:1]
    out_0 = yc + (np.maximum(np.minimum(y[:, unstriped(pos1)] - yc, f64(bound)[:1]), low) + np.maximum(np.minimum(y[:, unstriped(pos2)] - yc, f64(bound)[:1]), low) + np.maximum(np.minimum(y[:, unstriped(pos3)] - yc, f64(bound)[:1]), low) + np.maximum(np.minimum(y[:, unstriped(pos4)] - yc, f64(bound)[:1]), low)) / 4
    return (out_0,) + planes(out_0)

@@ -1,0 +1,204 @@
+from contextlib import ExitStack
+
+import concourse.mybir as mybir
+from concourse.masks import make_identity
+
+K, T, S, V, N = 512, 1024, 512, 256, 512
+D = 4
+P = 128
+PACK = 4
+FLOPS = 2 * K * N * S
+BYTES = 4 * (K * T + K * N + V + N * V) + N * V + N * V // 32 + 2 * P * (S + 5 * V) // 16
+
+F32 = mybir.dt.float32
+BF16 = mybir.dt.bfloat16
+U32 = mybir.dt.uint32
+I32 = mybir.dt.int32
+U16 = mybir.dt.uint16
+U8 = mybir.dt.uint8
+FP8X4 = mybir.dt.float8_e4m3fn_x4
+ALU = mybir.AluOpType
+COPY = mybir.ActivationFunctionType.Copy
+
+
+def tile_picked_huber_none_lo_kernel(
+    tc, xT, w1, bound, offs, cen, pos1, pos2, pos3, pos4, out_0, out_1, out_2
+):
+    nc = tc.nc
+    with ExitStack() as ctx:
+        keep = ctx.enter_context(tc.tile_pool(name="keep", bufs=1))
+        psum = ctx.enter_context(tc.psum_pool(name="psum", bufs=8))
+
+        def gather(on_vector, dst, window, offsets):
+            if on_vector:
+                nc.vector.tensor_copy(out=dst, in_=window.indirect(offsets))
+            else:
+                nc.scalar.activation(out=dst, in_=window.indirect(offsets), func=COPY)
+
+        x_rows = xT.rearrange("(p j) c -> p j c", j=PACK)
+        w_rows = w1.rearrange("(p j) c -> p j c", j=PACK)
+        x_plane = [keep.tile([P, T], F32, name=f"x_plane{j}") for j in range(PACK)]
+        w_half = [keep.tile([P, PACK, N // 2], F32, name=f"w_half{c}") for c in range(2)]
+        offs_sb = keep.tile([P, S // 16], U16)
+        cen_sb = keep.tile([P, V // 16], U16)
+        pos_sb = [keep.tile([P, V // 16], U16, name=f"pos_sb{d}") for d in range(D)]
+        reach = keep.tile([P, 2], F32)
+        neg_reach = keep.tile([P, 2], F32)
+
+        nc.sync.dma_start(out=x_plane[0][:], in_=x_rows[:, 0, :])
+        nc.sync.dma_start(offs_sb[:], offs)
+        for j in range(1, PACK):
+            nc.sync.dma_start(out=x_plane[j][:], in_=x_rows[:, j, :])
+        for c in range(2):
+            nc.sync.dma_start(out=w_half[c][:], in_=w_rows[:, :, c * 256 : (c + 1) * 256])
+        nc.sync.dma_start(cen_sb[:], cen)
+        for d, pos in enumerate((pos1, pos2, pos3, pos4)):
+            nc.sync.dma_start(pos_sb[d][:], pos)
+        with nc.allow_non_contiguous_dma(reason="one bound a partition"):
+            nc.sync.dma_start(out=reach[:], in_=bound[0, :].rearrange("(h p) -> p h", h=2))
+        ident = keep.tile([P, P], F32)
+        make_identity(nc, ident[:])
+        nc.gpsimd.tensor_scalar(out=neg_reach[:], in0=reach[:], scalar1=-1.0, scalar2=0.0, op0=ALU.mult, op1=ALU.add)
+
+        picked = keep.tile([P, PACK, S], BF16)
+        gather(False, picked[:, 0, :], x_plane[0][:], offs_sb[:])
+        gather(True, picked[:, 1, :], x_plane[1][:], offs_sb[:])
+        gather(False, picked[:, 2, :], x_plane[2][:], offs_sb[:])
+        gather(True, picked[:, 3, 0:256], x_plane[3][:], offs_sb[:, 0:16])
+        gather(False, picked[:, 3, 256:512], x_plane[3][:], offs_sb[:, 16:32])
+        x_woven = [keep.tile([P, S // 2, PACK], BF16, name=f"x_woven{h}", align_bytes=64) for h in range(2)]
+        x_codes = keep.tile([P, S], U32, align_bytes=64)
+        x_scales = keep.tile([P, S], U8, align_bytes=64)
+        for h in range(2):
+            nc.vector.tensor_copy(
+                out=x_woven[h][:].rearrange("p (c i) j -> p c j i", i=4),
+                in_=picked[:, :, h * 256 : (h + 1) * 256].rearrange("p j (c i) -> p c j i", i=4),
+            )
+        for h in range(2):
+            nc.vector.quantize_mx(
+                out=x_codes[:, h * 256 : (h + 1) * 256].bitcast(FP8X4),
+                scales=x_scales[:, h * 256 : (h + 1) * 256],
+                in_=x_woven[h][:].rearrange("p s j -> p (s j)"),
+            )
+
+        w_woven = [keep.tile([P, PACK, 64, PACK], BF16, name=f"w_woven{c}", align_bytes=64) for c in range(2)]
+        w_codes = [keep.tile([P, P], U32, name=f"w_codes{t}", align_bytes=64) for t in range(PACK)]
+        w_scales = [keep.tile([P, P], U8, name=f"w_scales{t}", align_bytes=64) for t in range(PACK)]
+        def weave_w(copy, c, m0, m1):
+            copy(
+                out=w_woven[c][:, :, m0:m1, :].rearrange("p t m j -> p m j t"),
+                in_=w_half[c][:, :, 4 * m0 : 4 * m1].rearrange("p j (m t) -> p m j t", t=PACK),
+            )
+
+        def quantize_w(c, t):
+            nc.vector.quantize_mx(
+                out=w_codes[t][:, c * 64 : (c + 1) * 64].bitcast(FP8X4),
+                scales=w_scales[t][:, c * 64 : (c + 1) * 64],
+                in_=w_woven[c][:, t, :, :].rearrange("p m j -> p (m j)"),
+            )
+
+        weave_w(nc.scalar.copy, 0, 0, 64)
+        for t in range(PACK):
+            quantize_w(0, t)
+        weave_w(nc.scalar.copy, 1, 0, 32)
+        weave_w(nc.vector.tensor_copy, 1, 32, 64)
+        for t in range(PACK):
+            quantize_w(1, t)
+
+        def product(t, s0, s1):
+            bank = psum.tile([P, S], F32, name=f"y_bank{t}_{s0}", tag="bank")
+            nc.tensor.matmul_mx(
+                out=bank[:, 0 : s1 - s0],
+                lhsT=w_codes[t][:].bitcast(FP8X4),
+                lhsT_scale=w_scales[t][:],
+                rhs=x_codes[:, s0:s1].bitcast(FP8X4),
+                rhs_scale=x_scales[:, s0:s1],
+                start=True,
+                stop=True,
+            )
+            return bank
+
+        y0_banks = [product(0, 0, 256), product(0, 256, 512)]
+        y_bank = [None] + [product(t, 0, S) for t in range(1, PACK)]
+        y_sb = [keep.tile([P, S], F32, name=f"y_sb{t}") for t in range(PACK)]
+        neg_centre = [keep.tile([P, V], F32, name=f"neg_centre{t}") for t in range(PACK)]
+        nbr = [[keep.tile([P, V], F32, name=f"nbr{t}_{d}") for d in range(D)] for t in range(PACK)]
+        pull = [[keep.tile([P, D, P], F32, name=f"pull{t}_{h}") for h in range(2)] for t in range(PACK)]
+        result = keep.tile([P, PACK, V], F32)
+        out_rows = out_0.rearrange("(p t) v -> p t v", t=PACK)
+        o_woven = [keep.tile([P, P, PACK], BF16, name=f"o_woven{h}", align_bytes=64) for h in range(2)]
+        o_codes = keep.tile([P, V], U32, align_bytes=64)
+        o_scales = keep.tile([P, V], U8, align_bytes=64)
+        out_words = out_1[0].rearrange("p v r -> p (v r)").bitcast(I32)
+
+        def fetch(t, vector_lists, v0=0, v1=V):
+            lc = slice(v0 // 16, v1 // 16)
+            nc.scalar.activation(out=neg_centre[t][:, v0:v1], in_=y_sb[t][:].indirect(cen_sb[:, lc]), func=COPY, scale=-1.0)
+            for d in range(D):
+                gather(d in vector_lists, nbr[t][d][:, v0:v1], y_sb[t][:], pos_sb[d][:, lc])
+
+        def clip(t, h):
+            cols = slice(h * P, (h + 1) * P)
+            diff = psum.tile([P, D, P], F32, name=f"diff{t}_{h}", tag="bank")
+            for d in range(D):
+                nc.tensor.matmul(diff[:, d, :], nbr[t][d][:, cols], ident[:], start=True, stop=False, is_transpose=True)
+                nc.tensor.matmul(diff[:, d, :], neg_centre[t][:, cols], ident[:], start=False, stop=True, is_transpose=True)
+            nc.vector.tensor_scalar(
+                out=pull[t][h][:], in0=diff[:], scalar1=reach[:, h : h + 1], scalar2=neg_reach[:, h : h + 1],
+                op0=ALU.min, op1=ALU.max,
+            )
+
+        def finish(t, halves):
+            total = psum.tile([P, S], F32, name=f"total{t}_{halves[0]}", tag="bank")
+            cols = slice(halves[0] * P, (halves[-1] + 1) * P)
+            for h in halves:
+                for d in range(D):
+                    nc.tensor.matmul(
+                        total[:, h * P : (h + 1) * P], pull[t][h][:, d, :], ident[:],
+                        start=(d == 0), stop=(d == D - 1), is_transpose=True,
+                    )
+            nc.vector.scalar_tensor_tensor(
+                out=result[:, t, cols], in0=total[:, cols], scalar=1.0 / D, in1=neg_centre[t][:, cols],
+                op0=ALU.mult, op1=ALU.subtract,
+            )
+            nc.sync.dma_start(out=out_rows[:, t, cols], in_=result[:, t, cols])
+
+        def planes(h, copy):
+            cols = slice(h * P, (h + 1) * P)
+            copy(
+                out=o_woven[h][:].rearrange("p (c i) t -> p c t i", i=4),
+                in_=result[:, :, cols].rearrange("p t (c i) -> p c t i", i=4),
+            )
+            nc.vector.quantize_mx(
+                out=o_codes[:, cols].bitcast(FP8X4), scales=o_scales[:, cols], in_=o_woven[h][:].rearrange("p v t -> p (v t)")
+            )
+            nc.sync.dma_start(out=out_words[:, cols], in_=o_codes[:, cols].bitcast(I32))
+
+        nc.scalar.copy(out=y_sb[0][:, 0:256], in_=y0_banks[0][:, 0:256])
+        nc.vector.tensor_copy(out=y_sb[0][:, 256:512], in_=y0_banks[1][:, 0:256])
+        fetch(0, (0, 1))
+        nc.vector.tensor_copy(out=y_sb[1][:], in_=y_bank[1][:])
+        nc.vector.tensor_copy(out=y_sb[2][:], in_=y_bank[2][:])
+        nc.vector.tensor_copy(out=y_sb[3][:], in_=y_bank[3][:])
+        fetch(1, (0,))
+        clip(0, 0)
+        clip(0, 1)
+        fetch(2, (0,))
+        finish(0, (0, 1))
+        clip(1, 0)
+        clip(1, 1)
+        fetch(3, (0,), 0, P)
+        fetch(3, (0,), P, V)
+        finish(1, (0, 1))
+        clip(2, 0)
+        clip(2, 1)
+        clip(3, 0)
+        finish(2, (0, 1))
+        finish(3, (0,))
+        clip(3, 1)
+        planes(0, nc.scalar.copy)
+        finish(3, (1,))
+        planes(1, nc.vector.tensor_copy)
+        for q in range(4):
+            queue = nc.scalar if q % 2 == 0 else nc.sync
+            queue.dma_start(out=out_2[0, 4 * q : 4 * q + 4, :].bitcast(I32), in_=o_scales[32 * q : 32 * q + 4, :].bitcast(I32))

@@ -27,7 +27,8 @@ def tile_picked_huber_none_lo_kernel(
     nc = tc.nc
     with ExitStack() as ctx:
         keep = ctx.enter_context(tc.tile_pool(name="keep", bufs=1))
-        psum = ctx.enter_context(tc.psum_pool(name="psum", bufs=8))
+        psum = ctx.enter_context(tc.psum_pool(name="psum", bufs=4))
+        psum_diff = ctx.enter_context(tc.psum_pool(name="psum_diff", bufs=4))
 
         def gather(on_vector, dst, window, offsets):
             if on_vector:
@@ -63,9 +64,9 @@ def tile_picked_huber_none_lo_kernel(
         picked = keep.tile([P, PACK, S], BF16)
         gather(False, picked[:, 0, :], x_plane[0][:], offs_sb[:])
         gather(True, picked[:, 1, :], x_plane[1][:], offs_sb[:])
-        gather(False, picked[:, 2, :], x_plane[2][:], offs_sb[:])
-        gather(True, picked[:, 3, 0:256], x_plane[3][:], offs_sb[:, 0:16])
-        gather(False, picked[:, 3, 256:512], x_plane[3][:], offs_sb[:, 16:32])
+        for j in (2, 3):
+            gather(True, picked[:, j, 0:256], x_plane[j][:], offs_sb[:, 0:16])
+            gather(False, picked[:, j, 256:512], x_plane[j][:], offs_sb[:, 16:32])
         x_woven = [keep.tile([P, S // 2, PACK], BF16, name=f"x_woven{h}", align_bytes=64) for h in range(2)]
         x_codes = keep.tile([P, S], U32, align_bytes=64)
         x_scales = keep.tile([P, S], U8, align_bytes=64)
@@ -81,29 +82,25 @@ def tile_picked_huber_none_lo_kernel(
                 in_=x_woven[h][:].rearrange("p s j -> p (s j)"),
             )
 
-        w_woven = [keep.tile([P, PACK, 64, PACK], BF16, name=f"w_woven{c}", align_bytes=64) for c in range(2)]
+        w_woven = keep.tile([P, PACK, P, PACK], BF16, align_bytes=64)
         w_codes = [keep.tile([P, P], U32, name=f"w_codes{t}", align_bytes=64) for t in range(PACK)]
         w_scales = [keep.tile([P, P], U8, name=f"w_scales{t}", align_bytes=64) for t in range(PACK)]
-        def weave_w(copy, c, m0, m1):
+        def weave_w(copy, m0, m1):
+            c, first = divmod(4 * m0, N // 2)
             copy(
-                out=w_woven[c][:, :, m0:m1, :].rearrange("p t m j -> p m j t"),
-                in_=w_half[c][:, :, 4 * m0 : 4 * m1].rearrange("p j (m t) -> p m j t", t=PACK),
+                out=w_woven[:, :, m0:m1, :].rearrange("p t m j -> p m j t"),
+                in_=w_half[c][:, :, first : first + 4 * (m1 - m0)].rearrange("p j (m t) -> p m j t", t=PACK),
             )
 
-        def quantize_w(c, t):
+        weave_w(nc.scalar.copy, 0, 64)
+        weave_w(nc.scalar.copy, 64, 96)
+        weave_w(nc.vector.tensor_copy, 96, 128)
+        for t in range(PACK):
             nc.vector.quantize_mx(
-                out=w_codes[t][:, c * 64 : (c + 1) * 64].bitcast(FP8X4),
-                scales=w_scales[t][:, c * 64 : (c + 1) * 64],
-                in_=w_woven[c][:, t, :, :].rearrange("p m j -> p (m j)"),
+                out=w_codes[t][:].bitcast(FP8X4),
+                scales=w_scales[t][:],
+                in_=w_woven[:, t, :, :].rearrange("p m j -> p (m j)"),
             )
-
-        weave_w(nc.scalar.copy, 0, 0, 64)
-        for t in range(PACK):
-            quantize_w(0, t)
-        weave_w(nc.scalar.copy, 1, 0, 32)
-        weave_w(nc.vector.tensor_copy, 1, 32, 64)
-        for t in range(PACK):
-            quantize_w(1, t)
 
         def product(t, s0, s1):
             bank = psum.tile([P, S], F32, name=f"y_bank{t}_{s0}", tag="bank")
@@ -119,7 +116,7 @@ def tile_picked_huber_none_lo_kernel(
             return bank
 
         y0_banks = [product(0, 0, 256), product(0, 256, 512)]
-        y_bank = [None] + [product(t, 0, S) for t in range(1, PACK)]
+        y_bank = {t: product(t, 0, S) for t in (1, 2)}
         y_sb = [keep.tile([P, S], F32, name=f"y_sb{t}") for t in range(PACK)]
         neg_centre = [keep.tile([P, V], F32, name=f"neg_centre{t}") for t in range(PACK)]
         nbr = [[keep.tile([P, V], F32, name=f"nbr{t}_{d}") for d in range(D)] for t in range(PACK)]
@@ -131,34 +128,53 @@ def tile_picked_huber_none_lo_kernel(
         o_scales = keep.tile([P, V], U8, align_bytes=64)
         out_words = out_1[0].rearrange("p v r -> p (v r)").bitcast(I32)
 
-        def fetch(t, vector_lists, v0=0, v1=V):
+        centred = set()
+
+        def fetch(t, vector_lists, gpsimd_lists=(), v0=0, v1=V):
             lc = slice(v0 // 16, v1 // 16)
             nc.scalar.activation(out=neg_centre[t][:, v0:v1], in_=y_sb[t][:].indirect(cen_sb[:, lc]), func=COPY, scale=-1.0)
             for d in range(D):
                 gather(d in vector_lists, nbr[t][d][:, v0:v1], y_sb[t][:], pos_sb[d][:, lc])
-
-        def clip(t, h):
-            cols = slice(h * P, (h + 1) * P)
-            diff = psum.tile([P, D, P], F32, name=f"diff{t}_{h}", tag="bank")
-            for d in range(D):
-                nc.tensor.matmul(diff[:, d, :], nbr[t][d][:, cols], ident[:], start=True, stop=False, is_transpose=True)
-                nc.tensor.matmul(diff[:, d, :], neg_centre[t][:, cols], ident[:], start=False, stop=True, is_transpose=True)
-            nc.vector.tensor_scalar(
-                out=pull[t][h][:], in0=diff[:], scalar1=reach[:, h : h + 1], scalar2=neg_reach[:, h : h + 1],
-                op0=ALU.min, op1=ALU.max,
-            )
-
-        def finish(t, halves):
-            total = psum.tile([P, S], F32, name=f"total{t}_{halves[0]}", tag="bank")
-            cols = slice(halves[0] * P, (halves[-1] + 1) * P)
-            for h in halves:
-                for d in range(D):
-                    nc.tensor.matmul(
-                        total[:, h * P : (h + 1) * P], pull[t][h][:, d, :], ident[:],
-                        start=(d == 0), stop=(d == D - 1), is_transpose=True,
+                if d in gpsimd_lists:
+                    nc.gpsimd.tensor_tensor(
+                        out=nbr[t][d][:, v0:v1], in0=nbr[t][d][:, v0:v1], in1=neg_centre[t][:, v0:v1], op=ALU.add
                     )
+                    centred.add((t, d))
+
+        def clip(t, halves):
+            diff = {h: psum_diff.tile([P, D, P], F32, name=f"diff{t}_{h}", tag="diff") for h in halves}
+            for d in range(D):
+                for h in halves:
+                    cols = slice(h * P, (h + 1) * P)
+                    alone = (t, d) in centred
+                    nc.tensor.matmul(diff[h][:, d, :], nbr[t][d][:, cols], ident[:], start=True, stop=alone, is_transpose=True)
+                    if not alone:
+                        nc.tensor.matmul(
+                            diff[h][:, d, :], neg_centre[t][:, cols], ident[:], start=False, stop=True, is_transpose=True
+                        )
+            for h in halves:
+                nc.vector.tensor_scalar(
+                    out=pull[t][h][:], in0=diff[h][:], scalar1=reach[:, h : h + 1], scalar2=neg_reach[:, h : h + 1],
+                    op0=ALU.min, op1=ALU.max,
+                )
+
+        totals = {}
+
+        def turn_back(t, h, fresh):
+            if fresh:
+                totals[t, h] = psum.tile([P, S], F32, name=f"total{t}_{h}", tag="bank")
+            else:
+                totals[t, h] = totals[t, h - 1]
+            for d in range(D):
+                nc.tensor.matmul(
+                    totals[t, h][:, h * P : (h + 1) * P], pull[t][h][:, d, :], ident[:],
+                    start=(d == 0), stop=(d == D - 1), is_transpose=True,
+                )
+
+        def finish(t, h0, h1):
+            cols = slice(h0 * P, h1 * P)
             nc.vector.scalar_tensor_tensor(
-                out=result[:, t, cols], in0=total[:, cols], scalar=1.0 / D, in1=neg_centre[t][:, cols],
+                out=result[:, t, cols], in0=totals[t, h0][:, cols], scalar=1.0 / D, in1=neg_centre[t][:, cols],
                 op0=ALU.mult, op1=ALU.subtract,
             )
             nc.sync.dma_start(out=out_rows[:, t, cols], in_=result[:, t, cols])
@@ -176,28 +192,34 @@ def tile_picked_huber_none_lo_kernel(
 
         nc.scalar.copy(out=y_sb[0][:, 0:256], in_=y0_banks[0][:, 0:256])
         nc.vector.tensor_copy(out=y_sb[0][:, 256:512], in_=y0_banks[1][:, 0:256])
+        y_bank[3] = product(3, 0, S)
         fetch(0, (0, 1))
         nc.vector.tensor_copy(out=y_sb[1][:], in_=y_bank[1][:])
+        fetch(1, (0, 1))
+        clip(0, (0, 1))
         nc.vector.tensor_copy(out=y_sb[2][:], in_=y_bank[2][:])
+        fetch(2, (0,), (0, 1))
         nc.vector.tensor_copy(out=y_sb[3][:], in_=y_bank[3][:])
-        fetch(1, (0,))
-        clip(0, 0)
-        clip(0, 1)
-        fetch(2, (0,))
-        finish(0, (0, 1))
-        clip(1, 0)
-        clip(1, 1)
-        fetch(3, (0,), 0, P)
-        fetch(3, (0,), P, V)
-        finish(1, (0, 1))
-        clip(2, 0)
-        clip(2, 1)
-        clip(3, 0)
-        finish(2, (0, 1))
-        finish(3, (0,))
-        clip(3, 1)
+        clip(1, (0, 1))
+        turn_back(0, 0, True)
+        turn_back(0, 1, False)
+        finish(0, 0, 2)
+        fetch(3, (), (0, 1), 0, P)
+        fetch(3, (), (0, 1), P, V)
+        clip(2, (0, 1))
+        turn_back(1, 0, True)
+        turn_back(1, 1, False)
+        finish(1, 0, 2)
+        clip(3, (0,))
+        turn_back(2, 0, True)
+        clip(3, (1,))
+        turn_back(2, 1, False)
+        finish(2, 0, 2)
+        turn_back(3, 0, True)
+        finish(3, 0, 1)
         planes(0, nc.scalar.copy)
-        finish(3, (1,))
+        turn_back(3, 1, True)
+        finish(3, 1, 2)
         planes(1, nc.vector.tensor_copy)
         for q in range(4):
             queue = nc.scalar if q % 2 == 0 else nc.sync

from contextlib import ExitStack

import concourse.mybir as mybir
from concourse.masks import make_identity

K, T, S, V, N = 512, 1024, 512, 256, 512
D = 4
P = 128
PACK = 4
FLOPS = 2 * K * N * S
BYTES = 4 * (K * T + K * N + V + N * V) + N * V + N * V // 32 + 2 * P * (S + 5 * V) // 16

F32 = mybir.dt.float32
BF16 = mybir.dt.bfloat16
U32 = mybir.dt.uint32
I32 = mybir.dt.int32
U16 = mybir.dt.uint16
U8 = mybir.dt.uint8
FP8X4 = mybir.dt.float8_e4m3fn_x4
ALU = mybir.AluOpType
COPY = mybir.ActivationFunctionType.Copy


def tile_picked_huber_none_lo_kernel(
    tc, xT, w1, bound, offs, cen, pos1, pos2, pos3, pos4, out_0, out_1, out_2
):
    nc = tc.nc
    with ExitStack() as ctx:
        keep = ctx.enter_context(tc.tile_pool(name="keep", bufs=1))
        psum = ctx.enter_context(tc.psum_pool(name="psum", bufs=4))
        psum_diff = ctx.enter_context(tc.psum_pool(name="psum_diff", bufs=4))

        def gather(on_vector, dst, window, offsets):
            if on_vector:
                nc.vector.tensor_copy(out=dst, in_=window.indirect(offsets))
            else:
                nc.scalar.activation(out=dst, in_=window.indirect(offsets), func=COPY)

        x_rows = xT.rearrange("(p j) c -> p j c", j=PACK)
        w_rows = w1.rearrange("(p j) c -> p j c", j=PACK)
        x_plane = [keep.tile([P, T], F32, name=f"x_plane{j}") for j in range(PACK)]
        w_half = [keep.tile([P, PACK, N // 2], F32, name=f"w_half{c}") for c in range(2)]
        offs_sb = keep.tile([P, S // 16], U16)
        cen_sb = keep.tile([P, V // 16], U16)
        pos_sb = [keep.tile([P, V // 16], U16, name=f"pos_sb{d}") for d in range(D)]
        reach = keep.tile([P, 2], F32)
        neg_reach = keep.tile([P, 2], F32)

        nc.sync.dma_start(out=x_plane[0][:], in_=x_rows[:, 0, :])
        nc.sync.dma_start(offs_sb[:], offs)
        for j in range(1, PACK):
            nc.sync.dma_start(out=x_plane[j][:], in_=x_rows[:, j, :])
        for c in range(2):
            nc.sync.dma_start(out=w_half[c][:], in_=w_rows[:, :, c * 256 : (c + 1) * 256])
        nc.sync.dma_start(cen_sb[:], cen)
        for d, pos in enumerate((pos1, pos2, pos3, pos4)):
            nc.sync.dma_start(pos_sb[d][:], pos)
        with nc.allow_non_contiguous_dma(reason="one bound a partition"):
            nc.sync.dma_start(out=reach[:], in_=bound[0, :].rearrange("(h p) -> p h", h=2))
        ident = keep.tile([P, P], F32)
        make_identity(nc, ident[:])
        nc.gpsimd.tensor_scalar(out=neg_reach[:], in0=reach[:], scalar1=-1.0, scalar2=0.0, op0=ALU.mult, op1=ALU.add)

        picked = keep.tile([P, PACK, S], BF16)
        gather(False, picked[:, 0, :], x_plane[0][:], offs_sb[:])
        gather(True, picked[:, 1, :], x_plane[1][:], offs_sb[:])
        for j in (2, 3):
            gather(True, picked[:, j, 0:256], x_plane[j][:], offs_sb[:, 0:16])
            gather(False, picked[:, j, 256:512], x_plane[j][:], offs_sb[:, 16:32])
        x_woven = [keep.tile([P, S // 2, PACK], BF16, name=f"x_woven{h}", align_bytes=64) for h in range(2)]
        x_codes = keep.tile([P, S], U32, align_bytes=64)
        x_scales = keep.tile([P, S], U8, align_bytes=64)
        for h in range(2):
            nc.vector.tensor_copy(
                out=x_woven[h][:].rearrange("p (c i) j -> p c j i", i=4),
                in_=picked[:, :, h * 256 : (h + 1) * 256].rearrange("p j (c i) -> p c j i", i=4),
            )
        for h in range(2):
            nc.vector.quantize_mx(
                out=x_codes[:, h * 256 : (h + 1) * 256].bitcast(FP8X4),
                scales=x_scales[:, h * 256 : (h + 1) * 256],
                in_=x_woven[h][:].rearrange("p s j -> p (s j)"),
            )

        w_woven = keep.tile([P, PACK, P, PACK], BF16, align_bytes=64)
        w_codes = [keep.tile([P, P], U32, name=f"w_codes{t}", align_bytes=64) for t in range(PACK)]
        w_scales = [keep.tile([P, P], U8, name=f"w_scales{t}", align_bytes=64) for t in range(PACK)]
        def weave_w(copy, m0, m1):
            c, first = divmod(4 * m0, N // 2)
            copy(
                out=w_woven[:, :, m0:m1, :].rearrange("p t m j -> p m j t"),
                in_=w_half[c][:, :, first : first + 4 * (m1 - m0)].rearrange("p j (m t) -> p m j t", t=PACK),
            )

        weave_w(nc.scalar.copy, 0, 64)
        weave_w(nc.scalar.copy, 64, 96)
        weave_w(nc.vector.tensor_copy, 96, 128)
        for t in range(PACK):
            nc.vector.quantize_mx(
                out=w_codes[t][:].bitcast(FP8X4),
                scales=w_scales[t][:],
                in_=w_woven[:, t, :, :].rearrange("p m j -> p (m j)"),
            )

        def product(t, s0, s1):
            bank = psum.tile([P, S], F32, name=f"y_bank{t}_{s0}", tag="bank")
            nc.tensor.matmul_mx(
                out=bank[:, 0 : s1 - s0],
                lhsT=w_codes[t][:].bitcast(FP8X4),
                lhsT_scale=w_scales[t][:],
                rhs=x_codes[:, s0:s1].bitcast(FP8X4),
                rhs_scale=x_scales[:, s0:s1],
                start=True,
                stop=True,
            )
            return bank

        y0_banks = [product(0, 0, 256), product(0, 256, 512)]
        y_bank = {t: product(t, 0, S) for t in (1, 2)}
        y_sb = [keep.tile([P, S], F32, name=f"y_sb{t}") for t in range(PACK)]
        neg_centre = [keep.tile([P, V], F32, name=f"neg_centre{t}") for t in range(PACK)]
        nbr = [[keep.tile([P, V], F32, name=f"nbr{t}_{d}") for d in range(D)] for t in range(PACK)]
        pull = [[keep.tile([P, D, P], F32, name=f"pull{t}_{h}") for h in range(2)] for t in range(PACK)]
        result = keep.tile([P, PACK, V], F32)
        out_rows = out_0.rearrange("(p t) v -> p t v", t=PACK)
        o_woven = [keep.tile([P, P, PACK], BF16, name=f"o_woven{h}", align_bytes=64) for h in range(2)]
        o_codes = keep.tile([P, V], U32, align_bytes=64)
        o_scales = keep.tile([P, V], U8, align_bytes=64)
        out_words = out_1[0].rearrange("p v r -> p (v r)").bitcast(I32)

        centred = set()

        def fetch(t, vector_lists, gpsimd_lists=(), v0=0, v1=V):
            lc = slice(v0 // 16, v1 // 16)
            nc.scalar.activation(out=neg_centre[t][:, v0:v1], in_=y_sb[t][:].indirect(cen_sb[:, lc]), func=COPY, scale=-1.0)
            for d in range(D):
                gather(d in vector_lists, nbr[t][d][:, v0:v1], y_sb[t][:], pos_sb[d][:, lc])
                if d in gpsimd_lists:
                    nc.gpsimd.tensor_tensor(
                        out=nbr[t][d][:, v0:v1], in0=nbr[t][d][:, v0:v1], in1=neg_centre[t][:, v0:v1], op=ALU.add
                    )
                    centred.add((t, d))

        def clip(t, halves):
            diff = {h: psum_diff.tile([P, D, P], F32, name=f"diff{t}_{h}", tag="diff") for h in halves}
            for d in range(D):
                for h in halves:
                    cols = slice(h * P, (h + 1) * P)
                    alone = (t, d) in centred
                    nc.tensor.matmul(diff[h][:, d, :], nbr[t][d][:, cols], ident[:], start=True, stop=alone, is_transpose=True)
                    if not alone:
                        nc.tensor.matmul(
                            diff[h][:, d, :], neg_centre[t][:, cols], ident[:], start=False, stop=True, is_transpose=True
                        )
            for h in halves:
                nc.vector.tensor_scalar(
                    out=pull[t][h][:], in0=diff[h][:], scalar1=reach[:, h : h + 1], scalar2=neg_reach[:, h : h + 1],
                    op0=ALU.min, op1=ALU.max,
                )

        totals = {}

        def turn_back(t, h, fresh):
            if fresh:
                totals[t, h] = psum.tile([P, S], F32, name=f"total{t}_{h}", tag="bank")
            else:
                totals[t, h] = totals[t, h - 1]
            for d in range(D):
                nc.tensor.matmul(
                    totals[t, h][:, h * P : (h + 1) * P], pull[t][h][:, d, :], ident[:],
                    start=(d == 0), stop=(d == D - 1), is_transpose=True,
                )

        def finish(t, h0, h1):
            cols = slice(h0 * P, h1 * P)
            nc.vector.scalar_tensor_tensor(
                out=result[:, t, cols], in0=totals[t, h0][:, cols], scalar=1.0 / D, in1=neg_centre[t][:, cols],
                op0=ALU.mult, op1=ALU.subtract,
            )
            nc.sync.dma_start(out=out_rows[:, t, cols], in_=result[:, t, cols])

        def planes(h, copy):
            cols = slice(h * P, (h + 1) * P)
            copy(
                out=o_woven[h][:].rearrange("p (c i) t -> p c t i", i=4),
                in_=result[:, :, cols].rearrange("p t (c i) -> p c t i", i=4),
            )
            nc.vector.quantize_mx(
                out=o_codes[:, cols].bitcast(FP8X4), scales=o_scales[:, cols], in_=o_woven[h][:].rearrange("p v t -> p (v t)")
            )
            nc.sync.dma_start(out=out_words[:, cols], in_=o_codes[:, cols].bitcast(I32))

        nc.scalar.copy(out=y_sb[0][:, 0:256], in_=y0_banks[0][:, 0:256])
        nc.vector.tensor_copy(out=y_sb[0][:, 256:512], in_=y0_banks[1][:, 0:256])
        y_bank[3] = product(3, 0, S)
        fetch(0, (0, 1))
        nc.vector.tensor_copy(out=y_sb[1][:], in_=y_bank[1][:])
        fetch(1, (0, 1))
        clip(0, (0, 1))
        nc.vector.tensor_copy(out=y_sb[2][:], in_=y_bank[2][:])
        fetch(2, (0,), (0, 1))
        nc.vector.tensor_copy(out=y_sb[3][:], in_=y_bank[3][:])
        clip(1, (0, 1))
        turn_back(0, 0, True)
        turn_back(0, 1, False)
        finish(0, 0, 2)
        fetch(3, (), (0, 1), 0, P)
        fetch(3, (), (0, 1), P, V)
        clip(2, (0, 1))
        turn_back(1, 0, True)
        turn_back(1, 1, False)
        finish(1, 0, 2)
        clip(3, (0,))
        turn_back(2, 0, True)
        clip(3, (1,))
        turn_back(2, 1, False)
        finish(2, 0, 2)
        turn_back(3, 0, True)
        finish(3, 0, 1)
        planes(0, nc.scalar.copy)
        turn_back(3, 1, True)
        finish(3, 1, 2)
        planes(1, nc.vector.tensor_copy)
        for q in range(4):
            queue = nc.scalar if q % 2 == 0 else nc.sync
            queue.dma_start(out=out_2[0, 4 * q : 4 * q + 4, :].bitcast(I32), in_=o_scales[32 * q : 32 * q + 4, :].bitcast(I32))
